import numpy as np
import ml_dtypes


def mxq(x, axis, fmt="e4m3"):
    dtype, down = {"e4m3": (ml_dtypes.float8_e4m3fn, 7), "e5m2": (ml_dtypes.float8_e5m2, 14)}[fmt]
    v = np.moveaxis(np.asarray(x, np.float32).astype(ml_dtypes.bfloat16).astype(np.float64), axis, -1)
    blocks = v.reshape(v.shape[:-1] + (-1, 32))
    amax = np.abs(blocks).max(-1, keepdims=True)
    byte = np.maximum(np.where(amax > 0, np.frexp(amax)[1] - 1 + 127, 0) - down, 1)
    scale = np.exp2(byte - 127.0)
    codes = (blocks / scale).astype(np.float32).astype(dtype).astype(np.float64)
    return np.moveaxis((codes * scale).reshape(v.shape), -1, axis)


WIDE = False


def mx_kscale(k):
    if not WIDE:
        return np.ones(k)
    levels = np.array([10, -10, 5, -5, 0])
    if k % 512:
        return np.exp2(np.random.permutation(np.resize(levels, k // 32))).repeat(32)
    a = np.empty((k // 512, 16))
    for p in range(k // 512):
        a[p, :8] = np.random.permutation(np.resize(levels, 8))
        for g in range(8):
            far = levels[np.abs(levels - a[p, g]) >= 10]
            a[p, g + 8] = far[np.random.randint(len(far))]
    return np.exp2(a.ravel()).repeat(32)


def f64(x):
    return np.asarray(x).astype(np.float64)


def striped(idx):
    return np.tile(idx.reshape(-1, 16).T, (8, 1)).astype(np.uint16)


def unstriped(offs):
    return offs[:16].T.reshape(-1).astype(np.int64)


def striped8(idx):
    return np.concatenate([x.reshape(-1, 16).T for x in idx]).astype(np.uint16)


def runs(offs, k):
    lists = np.stack([offs[16 * r : 16 * r + 16].T.reshape(-1) for r in range(8)]).astype(np.int64)
    return lists[np.arange(k) % 512 // 64]


def pack_weight(w):
    k, n = w.shape
    w = f64(np.asarray(w, np.float32).astype(ml_dtypes.bfloat16)).reshape(k // 32, 32, n)
    amax = np.abs(w).max(1)
    byte = np.clip(np.where(amax > 0, np.frexp(amax)[1] - 1 + 127 - 7, 1), 1, 254)
    scaled = (w * np.exp2(127.0 - byte)[:, None, :]).reshape(k, n).astype(np.float32)
    words = np.ascontiguousarray(scaled.reshape(k // 512, 128, 4, n).transpose(0, 1, 3, 2)).astype(ml_dtypes.float8_e4m3fn).view(np.uint8)
    return words, np.ascontiguousarray(byte.astype(np.uint8).reshape(k // 512, 16, n))


def unpack_weight(words, scales):
    g, p, n, _ = words.shape
    vals = np.ascontiguousarray(words).view(ml_dtypes.float8_e4m3fn).astype(np.float64) * np.repeat(np.exp2(scales.astype(np.float64) - 127.0), 8, axis=1)[..., None]
    return vals.transpose(0, 1, 3, 2).reshape(g * 512, n)


def sigmoid(v):
    return 1.0 / (1.0 + np.exp(-np.maximum(v, -700.0)))


K, T, S, N, H = 512, 2048, 512, 512, 512


def setup_inputs():
    n = np.random.standard_normal
    s = mx_kscale(K)[:, None]
    u = mx_kscale(S)
    packed_xT = pack_weight(n((K, T)) * s)
    return {
        "x_words": packed_xT[0],
        "x_scales": packed_xT[1],
        "wa": (n((K, H)) / np.sqrt(K) / s).astype(np.float32),
        "gt": (np.random.uniform(0.5, 1.5, (S, 1)) * u[:, None]).astype(np.float32),
        "w1": (n((S, N)) / np.sqrt(S) / u[:, None]).astype(np.float32),
        "offs": striped(np.random.permutation(T)[:S]),
        "n1": striped8(np.stack([np.random.permutation(H) for _ in range(8)])),
        "n2": striped8(np.stack([np.random.permutation(H) for _ in range(8)])),
        "n3": striped8(np.stack([np.random.permutation(H) for _ in range(8)])),
        "n4": striped8(np.stack([np.random.permutation(H) for _ in range(8)])),
    }


def reference(x_words, x_scales, wa, gt, w1, offs, n1, n2, n3, n4):
    xq = unpack_weight(x_words, x_scales)[:, unstriped(offs)]
    y = xq.T @ mxq(f64(wa), 0, "e4m3")
    sm = np.maximum(y, y[np.arange(S)[:, None], runs(n2, S)])
    ds = np.zeros((S, H))
    ds[np.arange(S)[:, None], runs(n1, S)] = sm
    z = f64(gt) * (ds * sigmoid(y))
    h = mxq(f64(w1), 0, "e4m3").T @ mxq(z, 0, "e4m3")
    return h[np.arange(N)[:, None], runs(n3, N)] - (h[np.arange(N)[:, None], runs(n4, N)])

@@ -1,0 +1,226 @@
+from contextlib import ExitStack
+
+import concourse.mybir as mybir
+
+K, T, S, N, H = 512, 2048, 512, 512, 512
+FLOPS = 2 * K * S * H + 2 * S * N * H
+
+F32 = mybir.dt.float32
+BF16 = mybir.dt.bfloat16
+I32 = mybir.dt.int32
+U32 = mybir.dt.uint32
+U16 = mybir.dt.uint16
+U8 = mybir.dt.uint8
+FP8X4 = mybir.dt.float8_e4m3fn_x4
+ALU = mybir.AluOpType
+ACT = mybir.ActivationFunctionType
+
+P = 128
+PACK = 4
+HALF = 256
+WIN = 1024
+VECTOR_COLS = 160
+LAST = PACK - 1
+
+
+def tile_picked_toksendggap_none_p_kernel(
+    tc, x_words, x_scales, wa, gt, w1, offs, n1, n2, n3, n4, out
+):
+    nc = tc.nc
+    with ExitStack() as ctx:
+        lists = ctx.enter_context(tc.tile_pool(name="lists", bufs=1))
+        keep = ctx.enter_context(tc.tile_pool(name="keep", bufs=1))
+        psum = ctx.enter_context(tc.psum_pool(name="psum", bufs=1))
+        halves = [slice(0, HALF), slice(HALF, H)]
+
+        def load_list(name, src):
+            tile = lists.tile([P, S // 16], U16, name=name)
+            nc.sync.dma_start(tile[:], src)
+            return tile
+
+        scale_table = keep.tile([P, T], U8, name="scale_table", align_bytes=64)
+        nc.vector.memset(scale_table[:].bitcast(I32), 0)
+        warm = keep.tile([P, 8], F32, name="warm")
+        nc.vector.memset(warm[:, 0:1], 0.0)
+
+        scale_rows = keep.tile([P, T // 4], I32, name="scale_rows")
+
+        def load_scales():
+            for q in range(4):
+                nc.sync.dma_start(
+                    scale_rows[32 * q : 32 * q + 4, :], x_scales[0, 4 * q : 4 * q + 4, :].bitcast(I32)
+                )
+
+        word_table = keep.tile([P, T], U32, name="word_table", align_bytes=64)
+        wa_rows = wa.rearrange("(p j) c -> p j c", j=PACK)
+        wa_raw = [keep.tile([P, PACK, HALF], F32, name="wa_raw%d" % u) for u in range(2)]
+        gt_t = keep.tile([P, PACK], F32, name="gt_t")
+        w1_raw = keep.tile([P, PACK, N], F32, name="w1_raw")
+        load_scales()
+        nc.sync.dma_start(word_table[:].bitcast(I32), x_words[0].rearrange("p n t -> p (n t)").bitcast(I32))
+        offs_t = load_list("offs_t", offs)
+        nc.sync.dma_start(wa_raw[0][:], wa_rows[:, :, halves[0]])
+        nc.sync.dma_start(wa_raw[1][:], wa_rows[:, :, halves[1]])
+        n2_t = load_list("n2_t", n2)
+        n1_t = load_list("n1_t", n1)
+        nc.sync.dma_start(gt_t[:], gt.rearrange("(p t) o -> p (t o)", t=PACK))
+        nc.sync.dma_start(w1_raw[:], w1.rearrange("(p j) c -> p j c", j=PACK))
+        n4_t = load_list("n4_t", n4)
+        n3_t = load_list("n3_t", n3)
+        nc.scalar.activation(warm[:, 4:5], warm[:, 0:1], ACT.Sigmoid)
+
+        for q in range(4):
+            nc.vector.tensor_copy(scale_table[32 * q : 32 * q + 4, :].bitcast(I32), scale_rows[32 * q : 32 * q + 4, :])
+        picked_bytes = keep.tile([P, S], U8, name="picked_bytes", align_bytes=64)
+        nc.vector.tensor_copy(picked_bytes[:], scale_table[:].indirect(offs_t[:]))
+        x_codes = keep.tile([P, S], U32, name="x_codes", align_bytes=64)
+        nc.vector.tensor_copy(
+            x_codes[:].rearrange("p (t m) -> p m t", t=PACK), word_table[:].indirect(offs_t[:])
+        )
+        x_bytes = keep.tile([P, S], U8, name="x_bytes", align_bytes=64)
+        nc.vector.tensor_copy(
+            x_bytes[:].rearrange("p (t m) -> p t m", t=PACK), picked_bytes[:].rearrange("p (m t) -> p t m", t=PACK)
+        )
+
+        def grouped_view(tile, lo, hi):
+            return tile[:, lo * PACK : hi * PACK].rearrange("p (c i j) -> p c j i", i=4, j=PACK)
+
+        def raw_view(tile, lo, hi):
+            return tile[:, :, lo:hi].rearrange("p j (c i) -> p c j i", i=4)
+
+        def quantize(name, grouped, width, tag=""):
+            codes = keep.tile([P, width], U32, name=name + "_codes", tag=tag, align_bytes=64)
+            scales = keep.tile([P, width], U8, name=name + "_bytes", align_bytes=64)
+            nc.vector.quantize_mx(out=codes[:].bitcast(FP8X4), scales=scales[:], in_=grouped)
+            return codes, scales
+
+        def product(bank, lhs, cols, rhs):
+            nc.tensor.matmul_mx(
+                out=bank,
+                lhsT=lhs[0][:, cols].bitcast(FP8X4),
+                lhsT_scale=lhs[1][:, cols],
+                rhs=rhs[0][:].bitcast(FP8X4),
+                rhs_scale=rhs[1][:],
+                start=True,
+                stop=True,
+            )
+
+        wa_grouped = [keep.tile([P, HALF * PACK], BF16, name="wa_grouped%d" % u, align_bytes=64) for u in range(2)]
+        nc.scalar.copy(grouped_view(wa_grouped[0], 0, HALF), raw_view(wa_raw[0], 0, HALF))
+        wa_q = [quantize("wa0", wa_grouped[0][:], HALF)]
+        nc.vector.tensor_copy(grouped_view(wa_grouped[1], 0, VECTOR_COLS), raw_view(wa_raw[1], 0, VECTOR_COLS))
+        nc.scalar.copy(grouped_view(wa_grouped[1], VECTOR_COLS, HALF), raw_view(wa_raw[1], VECTOR_COLS, HALF))
+        wa_q.append(quantize("wa1", wa_grouped[1][:], HALF))
+
+        rows = [keep.tile([P, WIN], F32, name="rows%d" % t) for t in range(PACK)]
+        sent = [keep.tile([P, WIN], F32, name="sent%d" % t, tag="sent%d" % t, align_bytes=64) for t in range(PACK)]
+        fetched = [keep.tile([P, H], F32, name="fetched%d" % t) for t in range(PACK)]
+        larger = [keep.tile([P, H], F32, name="larger%d" % t, tag="larger%d" % t, align_bytes=64) for t in range(PACK)]
+        z_grouped = [keep.tile([P, HALF, PACK], BF16, name="z_grouped%d" % u, align_bytes=64) for u in range(2)]
+
+        y_first = [psum.tile([P, HALF], F32, name="y_first%d" % u) for u in range(2)]
+        y_bank = [None] + [psum.tile([P, H], F32, name="y_bank%d" % t, tag="y_bank%d" % t) for t in range(1, PACK)]
+        x_q = (x_codes, x_bytes)
+        for u in range(2):
+            product(y_first[u][:], x_q, slice(0, P), wa_q[u])
+            nc.scalar.copy(rows[0][:, halves[u]], y_first[u][:])
+        for t in range(1, PACK):
+            for u in range(2):
+                product(y_bank[t][:, halves[u]], x_q, slice(t * P, (t + 1) * P), wa_q[u])
+            nc.scalar.copy(rows[t][:, 0:H], y_bank[t][:])
+        sig = [keep.tile([P, H], F32, name="sig%d" % t) for t in range(LAST)]
+        for u in range(2):
+            nc.scalar.activation(sig[0][:, halves[u]], y_first[u][:], ACT.Sigmoid)
+        for t in range(1, LAST):
+            nc.scalar.activation(sig[t][:], y_bank[t][:], ACT.Sigmoid)
+
+        w1_grouped = keep.tile([P, N * PACK], BF16, name="w1_grouped", align_bytes=64)
+        w1_dst = w1_grouped[:].rearrange("p (t m j) -> p m j t", t=PACK, j=PACK)
+        w1_src = w1_raw[:].rearrange("p j (m t) -> p m j t", t=PACK)
+        for u in range(2):
+            nc.scalar.copy(w1_dst[:, 64 * u : 64 * (u + 1)], w1_src[:, 64 * u : 64 * (u + 1)])
+
+        def fetch(t):
+            nc.vector.tensor_copy(fetched[t][:], rows[t][:].indirect(n2_t[:]))
+
+        def take_larger(t):
+            nc.vector.tensor_tensor(larger[t][:], fetched[t][:], rows[t][:, 0:H], ALU.max)
+
+        def send(t):
+            nc.vector.tensor_copy(sent[t][:].indirect(n1_t[:]), larger[t][:])
+
+        def gate(dst, t, cols):
+            nc.vector.scalar_tensor_tensor(
+                dst, sent[t][:, cols], gt_t[:, t : t + 1], sig[t][:, cols], ALU.mult, ALU.mult
+            )
+
+        def gate_and_weave(t):
+            z_plane = keep.tile([P, H], BF16, name="z_plane%d" % t, tag="z_plane%d" % t, align_bytes=64)
+            gate(z_plane[:], t, slice(0, H))
+            for u in range(2):
+                nc.scalar.copy(z_grouped[u][:, :, t], z_plane[:, halves[u]])
+
+        fetch(0)
+        fetch(1)
+        take_larger(0)
+        fetch(2)
+        send(0)
+        take_larger(1)
+        gate_and_weave(0)
+        send(1)
+        take_larger(2)
+        gate_and_weave(1)
+        fetch(3)
+        send(2)
+        take_larger(3)
+        gate_and_weave(2)
+        sig.append(keep.tile([P, H], F32, name="sig3", tag="z_plane2", align_bytes=64))
+        nc.scalar.activation(sig[LAST][:], y_bank[LAST][:], ACT.Sigmoid)
+        send(3)
+        w1_first = quantize("w1a", w1_grouped[:, 0 : P * PACK], P, tag="larger3")
+        z_last = keep.tile([P, HALF], BF16, name="z_last")
+        gate(z_last[:], LAST, halves[0])
+        nc.scalar.copy(z_grouped[0][:, :, LAST], z_last[:])
+        gate(z_grouped[1][:, :, LAST], LAST, halves[1])
+        z_q = [quantize("z%d" % u, z_grouped[u][:].rearrange("p c j -> p (c j)"), HALF) for u in range(2)]
+        w1_second = quantize("w1b", w1_grouped[:, P * PACK : 2 * P * PACK], P, tag="sent3")
+        w1_rest = quantize("w1c", w1_grouped[:, 2 * P * PACK :], 2 * P, tag="z_plane2")
+
+        h_first = [psum.tile([P, HALF], F32, name="h_first%d" % u) for u in range(2)]
+        product(h_first[0][:], w1_first, slice(0, P), z_q[0])
+        nc.scalar.copy(rows[0][:, halves[0]], h_first[0][:])
+        product(h_first[1][:], w1_first, slice(0, P), z_q[1])
+        nc.vector.tensor_copy(rows[0][:, halves[1]], h_first[1][:])
+        stationary = [None, (w1_second, slice(0, P)), (w1_rest, slice(0, P)), (w1_rest, slice(P, 2 * P))]
+        h_tags = [None, "h_bank1", "y_bank1", "y_bank2"]
+        for t in range(1, PACK):
+            h_bank = psum.tile([P, H], F32, name="h_bank%d" % t, tag=h_tags[t])
+            for u in range(2):
+                product(h_bank[:, halves[u]], stationary[t][0], stationary[t][1], z_q[u])
+            nc.scalar.copy(rows[t][:, 0:H], h_bank[:])
+
+        minus = [keep.tile([P, H], F32, name="minus%d" % t) for t in range(PACK)]
+        result = [keep.tile([P, H], F32, name="result%d" % t) for t in range(PACK)]
+        out_rows = out.rearrange("(p t) c -> p t c", t=PACK)
+
+        def fetch_minus(t):
+            nc.vector.tensor_copy(minus[t][:], rows[t][:].indirect(n4_t[:]))
+
+        def gap(t, lo, hi):
+            nc.vector.tensor_tensor(
+                result[t][:, lo:hi],
+                rows[t][:].indirect(n3_t[:, lo // 16 : hi // 16]),
+                minus[t][:, lo:hi],
+                ALU.subtract,
+            )
+            nc.sync.dma_start(out_rows[:, t, lo:hi], result[t][:, lo:hi])
+
+        fetch_minus(0)
+        fetch_minus(1)
+        gap(0, 0, H)
+        fetch_minus(2)
+        gap(1, 0, H)
+        fetch_minus(3)
+        gap(2, 0, H)
+        gap(3, 0, HALF)
+        gap(3, HALF, H)

@@ -53,14 +53,16 @@ def tile_picked_toksendggap_none_p_kernel(
 
         word_table = keep.tile([P, T], U32, name="word_table", align_bytes=64)
         wa_rows = wa.rearrange("(p j) c -> p j c", j=PACK)
-        wa_raw = [keep.tile([P, PACK, HALF], F32, name="wa_raw%d" % u) for u in range(2)]
+        chunks = [slice(0, 256), slice(256, 384), slice(384, 512)]
+        wa_raw = [keep.tile([P, PACK, c.stop - c.start], F32, name="wa_raw%d" % c.start) for c in chunks]
         gt_t = keep.tile([P, PACK], F32, name="gt_t")
         w1_raw = keep.tile([P, PACK, N], F32, name="w1_raw")
         load_scales()
         nc.sync.dma_start(word_table[:].bitcast(I32), x_words[0].rearrange("p n t -> p (n t)").bitcast(I32))
         offs_t = load_list("offs_t", offs)
-        nc.sync.dma_start(wa_raw[0][:], wa_rows[:, :, halves[0]])
-        nc.sync.dma_start(wa_raw[1][:], wa_rows[:, :, halves[1]])
+        nc.sync.dma_start(wa_raw[0][:], wa_rows[:, :, chunks[0]])
+        nc.sync.dma_start(wa_raw[1][:], wa_rows[:, :, chunks[1]])
+        nc.sync.dma_start(wa_raw[2][:], wa_rows[:, :, chunks[2]])
         n2_t = load_list("n2_t", n2)
         n1_t = load_list("n1_t", n1)
         nc.sync.dma_start(gt_t[:], gt.rearrange("(p t) o -> p (t o)", t=PACK))
@@ -105,34 +107,32 @@ def tile_picked_toksendggap_none_p_kernel(
                 stop=True,
             )
 
-        wa_grouped = [keep.tile([P, HALF * PACK], BF16, name="wa_grouped%d" % u, align_bytes=64) for u in range(2)]
-        nc.scalar.copy(grouped_view(wa_grouped[0], 0, HALF), raw_view(wa_raw[0], 0, HALF))
-        wa_q = [quantize("wa0", wa_grouped[0][:], HALF)]
-        nc.vector.tensor_copy(grouped_view(wa_grouped[1], 0, VECTOR_COLS), raw_view(wa_raw[1], 0, VECTOR_COLS))
-        nc.scalar.copy(grouped_view(wa_grouped[1], VECTOR_COLS, HALF), raw_view(wa_raw[1], VECTOR_COLS, HALF))
-        wa_q.append(quantize("wa1", wa_grouped[1][:], HALF))
+        wa_codes = keep.tile([P, H], U32, name="wa_codes", align_bytes=64)
+        wa_bytes = keep.tile([P, H], U8, name="wa_bytes", align_bytes=64)
+        for u, c in enumerate(chunks):
+            width = c.stop - c.start
+            grouped = keep.tile([P, width * PACK], BF16, name="wa_grouped%d" % u, align_bytes=64)
+            nc.scalar.copy(grouped_view(grouped, 0, width), raw_view(wa_raw[u], 0, width))
+            nc.vector.quantize_mx(out=wa_codes[:, c].bitcast(FP8X4), scales=wa_bytes[:, c], in_=grouped[:])
 
         rows = [keep.tile([P, WIN], F32, name="rows%d" % t) for t in range(PACK)]
         sent = [keep.tile([P, WIN], F32, name="sent%d" % t, tag="sent%d" % t, align_bytes=64) for t in range(PACK)]
         fetched = [keep.tile([P, H], F32, name="fetched%d" % t) for t in range(PACK)]
-        larger = [keep.tile([P, H], F32, name="larger%d" % t, tag="larger%d" % t, align_bytes=64) for t in range(PACK)]
+        larger = {}
         z_grouped = [keep.tile([P, HALF, PACK], BF16, name="z_grouped%d" % u, align_bytes=64) for u in range(2)]
 
-        y_first = [psum.tile([P, HALF], F32, name="y_first%d" % u) for u in range(2)]
+        y_first = [psum.tile([P, H], F32, name="y_first%d" % u) for u in range(2)]
         y_bank = [None] + [psum.tile([P, H], F32, name="y_bank%d" % t, tag="y_bank%d" % t) for t in range(1, PACK)]
         x_q = (x_codes, x_bytes)
-        for u in range(2):
-            product(y_first[u][:], x_q, slice(0, P), wa_q[u])
-            nc.scalar.copy(rows[0][:, halves[u]], y_first[u][:])
+        for u, c in enumerate(chunks):
+            product(y_first[u % 2][:, c], x_q, slice(0, P), (wa_codes[:, c], wa_bytes[:, c]))
+            nc.scalar.copy(rows[0][:, c], y_first[u % 2][:, c])
         for t in range(1, PACK):
-            for u in range(2):
-                product(y_bank[t][:, halves[u]], x_q, slice(t * P, (t + 1) * P), wa_q[u])
+            product(y_bank[t][:], x_q, slice(t * P, (t + 1) * P), (wa_codes, wa_bytes))
             nc.scalar.copy(rows[t][:, 0:H], y_bank[t][:])
-        sig = [keep.tile([P, H], F32, name="sig%d" % t) for t in range(LAST)]
-        for u in range(2):
-            nc.scalar.activation(sig[0][:, halves[u]], y_first[u][:], ACT.Sigmoid)
-        for t in range(1, LAST):
-            nc.scalar.activation(sig[t][:], y_bank[t][:], ACT.Sigmoid)
+        sig = [keep.tile([P, H], F32, name="sig%d" % t, tag="sig%d" % t, align_bytes=64) for t in range(LAST)]
+        for t in range(LAST):
+            nc.scalar.activation(sig[t][:], rows[t][:, 0:H], ACT.Sigmoid)
 
         w1_grouped = keep.tile([P, N * PACK], BF16, name="w1_grouped", align_bytes=64)
         w1_dst = w1_grouped[:].rearrange("p (t m j) -> p m j t", t=PACK, j=PACK)
@@ -144,7 +144,8 @@ def tile_picked_toksendggap_none_p_kernel(
             nc.vector.tensor_copy(fetched[t][:], rows[t][:].indirect(n2_t[:]))
 
         def take_larger(t):
-            nc.vector.tensor_tensor(larger[t][:], fetched[t][:], rows[t][:, 0:H], ALU.max)
+            larger[t] = keep.tile([P, H], F32, name="larger%d" % t, tag="larger%d" % min(t, 2), align_bytes=64)
+            nc.vector.tensor_tensor(larger[t][:], fetched[t][:], (y_bank[t][:] if t else rows[t][:, 0:H]), ALU.max)
 
         def send(t):
             nc.vector.tensor_copy(sent[t][:].indirect(n1_t[:]), larger[t][:])
@@ -155,10 +156,10 @@ def tile_picked_toksendggap_none_p_kernel(
             )
 
         def gate_and_weave(t):
-            z_plane = keep.tile([P, H], BF16, name="z_plane%d" % t, tag="z_plane%d" % t, align_bytes=64)
-            gate(z_plane[:], t, slice(0, H))
+            z_plane = keep.tile([P, H], F32, name="z_plane%d" % t, tag="z_plane%d" % t, align_bytes=64)
             for u in range(2):
-                nc.scalar.copy(z_grouped[u][:, :, t], z_plane[:, halves[u]])
+                nc.gpsimd.tensor_tensor(z_plane[:, halves[u]], sent[t][:, halves[u]], sig[t][:, halves[u]], ALU.mult)
+                nc.scalar.activation(z_grouped[u][:, :, t], z_plane[:, halves[u]], ACT.Copy, scale=gt_t[:, t : t + 1])
 
         fetch(0)
         fetch(1)
@@ -175,15 +176,15 @@ def tile_picked_toksendggap_none_p_kernel(
         take_larger(3)
         gate_and_weave(2)
         sig.append(keep.tile([P, H], F32, name="sig3", tag="z_plane2", align_bytes=64))
-        nc.scalar.activation(sig[LAST][:], y_bank[LAST][:], ACT.Sigmoid)
+        nc.scalar.activation(sig[LAST][:], rows[LAST][:, 0:H], ACT.Sigmoid)
         send(3)
-        w1_first = quantize("w1a", w1_grouped[:, 0 : P * PACK], P, tag="larger3")
-        z_last = keep.tile([P, HALF], BF16, name="z_last")
+        w1_first = quantize("w1a", w1_grouped[:, 0 : P * PACK], P, tag="larger2")
+        z_last = keep.tile([P, HALF], BF16, name="z_last", tag="z_last", align_bytes=64)
         gate(z_last[:], LAST, halves[0])
         nc.scalar.copy(z_grouped[0][:, :, LAST], z_last[:])
         gate(z_grouped[1][:, :, LAST], LAST, halves[1])
         z_q = [quantize("z%d" % u, z_grouped[u][:].rearrange("p c j -> p (c j)"), HALF) for u in range(2)]
-        w1_second = quantize("w1b", w1_grouped[:, P * PACK : 2 * P * PACK], P, tag="sent3")
+        w1_second = quantize("w1b", w1_grouped[:, P * PACK : 2 * P * PACK], P, tag="z_last")
         w1_rest = quantize("w1c", w1_grouped[:, 2 * P * PACK :], 2 * P, tag="z_plane2")
 
         h_first = [psum.tile([P, HALF], F32, name="h_first%d" % u) for u in range(2)]

@@ -17,10 +17,15 @@ ACT = mybir.ActivationFunctionType
 
 P = 128
 PACK = 4
-HALF = 256
-WIN = 1024
-VECTOR_COLS = 160
 LAST = PACK - 1
+QUADRANT = 32
+LIST_ROWS = 16
+ALIGN = 64
+WINDOW = 2 * H
+HALVES = [slice(0, H // 2), slice(H // 2, H)]
+QUARTERS = [slice(c, c + H // 4) for c in range(0, H, H // 4)]
+WA_CHUNKS = [slice(0, 256), slice(256, 384), slice(384, 512)]
+GPSIMD_COLS = 96
 
 
 def tile_picked_toksendggap_none_p_kernel(
@@ -31,197 +36,193 @@ def tile_picked_toksendggap_none_p_kernel(
         lists = ctx.enter_context(tc.tile_pool(name="lists", bufs=1))
         keep = ctx.enter_context(tc.tile_pool(name="keep", bufs=1))
         psum = ctx.enter_context(tc.psum_pool(name="psum", bufs=1))
-        halves = [slice(0, HALF), slice(HALF, H)]
+
+        def sbuf(name, shape, dtype, tag=""):
+            return keep.tile([P] + shape, dtype, name=name, tag=tag or name, align_bytes=ALIGN)
 
         def load_list(name, src):
-            tile = lists.tile([P, S // 16], U16, name=name)
+            tile = lists.tile([P, S // LIST_ROWS], U16, name=name)
             nc.sync.dma_start(tile[:], src)
             return tile
 
-        scale_table = keep.tile([P, T], U8, name="scale_table", align_bytes=64)
-        nc.vector.memset(scale_table[:].bitcast(I32), 0)
-        warm = keep.tile([P, 8], F32, name="warm")
-        nc.vector.memset(warm[:, 0:1], 0.0)
+        def scale_partitions(q):
+            return slice(QUADRANT * q, QUADRANT * q + 4)
 
-        scale_rows = keep.tile([P, T // 4], I32, name="scale_rows")
+        def quantize(codes, scales, grouped):
+            nc.vector.quantize_mx(out=codes.bitcast(FP8X4), scales=scales, in_=grouped)
 
-        def load_scales():
-            for q in range(4):
-                nc.sync.dma_start(
-                    scale_rows[32 * q : 32 * q + 4, :], x_scales[0, 4 * q : 4 * q + 4, :].bitcast(I32)
-                )
-
-        word_table = keep.tile([P, T], U32, name="word_table", align_bytes=64)
-        wa_rows = wa.rearrange("(p j) c -> p j c", j=PACK)
-        chunks = [slice(0, 256), slice(256, 384), slice(384, 512)]
-        wa_raw = [keep.tile([P, PACK, c.stop - c.start], F32, name="wa_raw%d" % c.start) for c in chunks]
-        gt_t = keep.tile([P, PACK], F32, name="gt_t")
-        w1_raw = keep.tile([P, PACK, N], F32, name="w1_raw")
-        load_scales()
-        nc.sync.dma_start(word_table[:].bitcast(I32), x_words[0].rearrange("p n t -> p (n t)").bitcast(I32))
-        offs_t = load_list("offs_t", offs)
-        nc.sync.dma_start(wa_raw[0][:], wa_rows[:, :, chunks[0]])
-        nc.sync.dma_start(wa_raw[1][:], wa_rows[:, :, chunks[1]])
-        nc.sync.dma_start(wa_raw[2][:], wa_rows[:, :, chunks[2]])
-        n2_t = load_list("n2_t", n2)
-        n1_t = load_list("n1_t", n1)
-        nc.sync.dma_start(gt_t[:], gt.rearrange("(p t) o -> p (t o)", t=PACK))
-        nc.sync.dma_start(w1_raw[:], w1.rearrange("(p j) c -> p j c", j=PACK))
-        n4_t = load_list("n4_t", n4)
-        n3_t = load_list("n3_t", n3)
-        nc.scalar.activation(warm[:, 4:5], warm[:, 0:1], ACT.Sigmoid)
-
-        for q in range(4):
-            nc.vector.tensor_copy(scale_table[32 * q : 32 * q + 4, :].bitcast(I32), scale_rows[32 * q : 32 * q + 4, :])
-        picked_bytes = keep.tile([P, S], U8, name="picked_bytes", align_bytes=64)
-        nc.vector.tensor_copy(picked_bytes[:], scale_table[:].indirect(offs_t[:]))
-        x_codes = keep.tile([P, S], U32, name="x_codes", align_bytes=64)
-        nc.vector.tensor_copy(
-            x_codes[:].rearrange("p (t m) -> p m t", t=PACK), word_table[:].indirect(offs_t[:])
-        )
-        x_bytes = keep.tile([P, S], U8, name="x_bytes", align_bytes=64)
-        nc.vector.tensor_copy(
-            x_bytes[:].rearrange("p (t m) -> p t m", t=PACK), picked_bytes[:].rearrange("p (m t) -> p t m", t=PACK)
-        )
-
-        def grouped_view(tile, lo, hi):
-            return tile[:, lo * PACK : hi * PACK].rearrange("p (c i j) -> p c j i", i=4, j=PACK)
-
-        def raw_view(tile, lo, hi):
-            return tile[:, :, lo:hi].rearrange("p j (c i) -> p c j i", i=4)
-
-        def quantize(name, grouped, width, tag=""):
-            codes = keep.tile([P, width], U32, name=name + "_codes", tag=tag, align_bytes=64)
-            scales = keep.tile([P, width], U8, name=name + "_bytes", align_bytes=64)
-            nc.vector.quantize_mx(out=codes[:].bitcast(FP8X4), scales=scales[:], in_=grouped)
-            return codes, scales
-
-        def product(bank, lhs, cols, rhs):
+        def product(bank, lhs_codes, lhs_scales, rhs_codes, rhs_scales):
             nc.tensor.matmul_mx(
                 out=bank,
-                lhsT=lhs[0][:, cols].bitcast(FP8X4),
-                lhsT_scale=lhs[1][:, cols],
-                rhs=rhs[0][:].bitcast(FP8X4),
-                rhs_scale=rhs[1][:],
+                lhsT=lhs_codes.bitcast(FP8X4),
+                lhsT_scale=lhs_scales,
+                rhs=rhs_codes.bitcast(FP8X4),
+                rhs_scale=rhs_scales,
                 start=True,
                 stop=True,
             )
 
-        wa_codes = keep.tile([P, H], U32, name="wa_codes", align_bytes=64)
-        wa_bytes = keep.tile([P, H], U8, name="wa_bytes", align_bytes=64)
-        for u, c in enumerate(chunks):
-            width = c.stop - c.start
-            grouped = keep.tile([P, width * PACK], BF16, name="wa_grouped%d" % u, align_bytes=64)
-            nc.scalar.copy(grouped_view(grouped, 0, width), raw_view(wa_raw[u], 0, width))
-            nc.vector.quantize_mx(out=wa_codes[:, c].bitcast(FP8X4), scales=wa_bytes[:, c], in_=grouped[:])
+        scale_table = sbuf("scale_table", [T], U8)
+        nc.vector.memset(scale_table[:].bitcast(I32), 0)
+        warm = sbuf("warm", [8], F32)
+        nc.vector.memset(warm[:, 0:1], 0.0)
 
-        rows = [keep.tile([P, WIN], F32, name="rows%d" % t) for t in range(PACK)]
-        sent = [keep.tile([P, WIN], F32, name="sent%d" % t, tag="sent%d" % t, align_bytes=64) for t in range(PACK)]
-        fetched = [keep.tile([P, H], F32, name="fetched%d" % t) for t in range(PACK)]
-        larger = {}
-        z_grouped = [keep.tile([P, HALF, PACK], BF16, name="z_grouped%d" % u, align_bytes=64) for u in range(2)]
+        scale_rows = sbuf("scale_rows", [T // 4], I32)
+        for q in range(4):
+            nc.sync.dma_start(scale_rows[scale_partitions(q), :], x_scales[0, 4 * q : 4 * q + 4, :].bitcast(I32))
+        word_table = sbuf("word_table", [T], U32)
+        nc.sync.dma_start(word_table[:].bitcast(I32), x_words[0].rearrange("p n t -> p (n t)").bitcast(I32))
+        offs_t = load_list("offs_t", offs)
+        wa_rows = wa.rearrange("(p j) c -> p j c", j=PACK)
+        wa_raw = []
+        for u, cols in enumerate(WA_CHUNKS):
+            wa_raw.append(sbuf("wa_raw%d" % u, [PACK, cols.stop - cols.start], F32))
+            nc.sync.dma_start(wa_raw[u][:], wa_rows[:, :, cols])
+        n2_t = load_list("n2_t", n2)
+        n1_t = load_list("n1_t", n1)
+        gt_t = sbuf("gt_t", [PACK], F32)
+        nc.sync.dma_start(gt_t[:], gt.rearrange("(p t) o -> p (t o)", t=PACK))
+        w1_raw = sbuf("w1_raw", [PACK, N], F32)
+        nc.sync.dma_start(w1_raw[:], w1.rearrange("(p j) c -> p j c", j=PACK))
+        n4_t = load_list("n4_t", n4)
+        n3_t = load_list("n3_t", n3)
 
-        y_first = [psum.tile([P, H], F32, name="y_first%d" % u) for u in range(2)]
-        y_bank = [None] + [psum.tile([P, H], F32, name="y_bank%d" % t, tag="y_bank%d" % t) for t in range(1, PACK)]
-        x_q = (x_codes, x_bytes)
-        for u, c in enumerate(chunks):
-            product(y_first[u % 2][:, c], x_q, slice(0, P), (wa_codes[:, c], wa_bytes[:, c]))
-            nc.scalar.copy(rows[0][:, c], y_first[u % 2][:, c])
+        nc.scalar.activation(warm[:, 4:5], warm[:, 0:1], ACT.Sigmoid)
+
+        for q in range(4):
+            nc.vector.tensor_copy(scale_table[scale_partitions(q), :].bitcast(I32), scale_rows[scale_partitions(q), :])
+        picked_scales = sbuf("picked_scales", [S], U8)
+        nc.vector.tensor_copy(picked_scales[:], scale_table[:].indirect(offs_t[:]))
+        x_codes = sbuf("x_codes", [S], U32)
+        nc.vector.tensor_copy(x_codes[:].rearrange("p (t m) -> p m t", t=PACK), word_table[:].indirect(offs_t[:]))
+        x_scale = sbuf("x_scale", [S], U8)
+        nc.vector.tensor_copy(
+            x_scale[:].rearrange("p (t m) -> p t m", t=PACK), picked_scales[:].rearrange("p (m t) -> p t m", t=PACK)
+        )
+
+        wa_codes = sbuf("wa_codes", [H], U32)
+        wa_scale = sbuf("wa_scale", [H], U8)
+        for u, cols in enumerate(WA_CHUNKS):
+            grouped = sbuf("wa_grouped%d" % u, [(cols.stop - cols.start) * PACK], BF16)
+            dst = grouped[:].rearrange("p (c i j) -> p c j i", i=4, j=PACK)
+            src = wa_raw[u][:].rearrange("p j (c i) -> p c j i", i=4)
+            shared = GPSIMD_COLS // 4 if u == 0 else 0
+            if shared:
+                nc.gpsimd.tensor_scalar(dst[:, :shared], src[:, :shared], 1.0, 0.0, ALU.mult, ALU.add)
+            nc.scalar.copy(dst[:, shared:], src[:, shared:])
+            quantize(wa_codes[:, cols], wa_scale[:, cols], grouped[:])
+
+        rows = [sbuf("rows%d" % t, [WINDOW], F32) for t in range(PACK)]
+        for u, cols in enumerate(WA_CHUNKS):
+            y_chunk = psum.tile([P, cols.stop - cols.start], F32, name="y_chunk%d" % u, tag="chunk%d" % u)
+            product(y_chunk[:], x_codes[:, 0:P], x_scale[:, 0:P], wa_codes[:, cols], wa_scale[:, cols])
+            nc.scalar.copy(rows[0][:, cols], y_chunk[:])
+        y_bank = {}
         for t in range(1, PACK):
-            product(y_bank[t][:], x_q, slice(t * P, (t + 1) * P), (wa_codes, wa_bytes))
+            tokens = slice(t * P, (t + 1) * P)
+            y_bank[t] = psum.tile([P, H], F32, name="y_bank%d" % t, tag="bank%d" % t)
+            product(y_bank[t][:], x_codes[:, tokens], x_scale[:, tokens], wa_codes[:], wa_scale[:])
             nc.scalar.copy(rows[t][:, 0:H], y_bank[t][:])
-        sig = [keep.tile([P, H], F32, name="sig%d" % t, tag="sig%d" % t, align_bytes=64) for t in range(LAST)]
+        sig = [sbuf("sig%d" % t, [H], F32) for t in range(LAST)]
         for t in range(LAST):
             nc.scalar.activation(sig[t][:], rows[t][:, 0:H], ACT.Sigmoid)
 
-        w1_grouped = keep.tile([P, N * PACK], BF16, name="w1_grouped", align_bytes=64)
+        w1_grouped = sbuf("w1_grouped", [N * PACK], BF16)
         w1_dst = w1_grouped[:].rearrange("p (t m j) -> p m j t", t=PACK, j=PACK)
         w1_src = w1_raw[:].rearrange("p j (m t) -> p m j t", t=PACK)
-        for u in range(2):
-            nc.scalar.copy(w1_dst[:, 64 * u : 64 * (u + 1)], w1_src[:, 64 * u : 64 * (u + 1)])
+        for m0 in range(0, P, P // 2):
+            nc.scalar.copy(w1_dst[:, m0 : m0 + P // 2], w1_src[:, m0 : m0 + P // 2])
+
+        def quantize_w1(first, count, tag):
+            codes = sbuf("w1_codes%d" % first, [count * P], U32, tag)
+            scales = sbuf("w1_scale%d" % first, [count * P], U8)
+            quantize(codes[:], scales[:], w1_grouped[:, first * P * PACK : (first + count) * P * PACK])
+            return [(codes[:, c * P : (c + 1) * P], scales[:, c * P : (c + 1) * P]) for c in range(count)]
+
+        fetched, larger = {}, {}
+        sent = [sbuf("sent%d" % t, [WINDOW], F32) for t in range(PACK)]
+        z_grouped = [sbuf("z_grouped%d" % u, [H // 2, PACK], BF16) for u in range(2)]
 
         def fetch(t):
+            fetched[t] = sbuf("fetched%d" % t, [H], F32, "fetched%d" % (t % 2))
             nc.vector.tensor_copy(fetched[t][:], rows[t][:].indirect(n2_t[:]))
 
         def take_larger(t):
-            larger[t] = keep.tile([P, H], F32, name="larger%d" % t, tag="larger%d" % min(t, 2), align_bytes=64)
-            nc.vector.tensor_tensor(larger[t][:], fetched[t][:], (y_bank[t][:] if t else rows[t][:, 0:H]), ALU.max)
+            larger[t] = sbuf("larger%d" % t, [H], F32, "larger%d" % (t % 2))
+            nc.vector.tensor_tensor(larger[t][:], fetched[t][:], y_bank[t][:] if t else rows[0][:, 0:H], ALU.max)
 
         def send(t):
             nc.vector.tensor_copy(sent[t][:].indirect(n1_t[:]), larger[t][:])
 
-        def gate(dst, t, cols):
-            nc.vector.scalar_tensor_tensor(
-                dst, sent[t][:, cols], gt_t[:, t : t + 1], sig[t][:, cols], ALU.mult, ALU.mult
-            )
+        def gate_beside(t):
+            gated = sbuf("gated%d" % t, [H], F32)
+            for u, cols in enumerate(HALVES):
+                nc.gpsimd.tensor_tensor(gated[:, cols], sent[t][:, cols], sig[t][:, cols], ALU.mult)
+                nc.scalar.activation(z_grouped[u][:, :, t], gated[:, cols], ACT.Copy, scale=gt_t[:, t : t + 1])
 
-        def gate_and_weave(t):
-            z_plane = keep.tile([P, H], F32, name="z_plane%d" % t, tag="z_plane%d" % t, align_bytes=64)
-            for u in range(2):
-                nc.gpsimd.tensor_tensor(z_plane[:, halves[u]], sent[t][:, halves[u]], sig[t][:, halves[u]], ALU.mult)
-                nc.scalar.activation(z_grouped[u][:, :, t], z_plane[:, halves[u]], ACT.Copy, scale=gt_t[:, t : t + 1])
+        def gate_last(dst, cols):
+            nc.vector.scalar_tensor_tensor(
+                dst, sent[LAST][:, cols], gt_t[:, LAST : LAST + 1], sig[LAST][:, cols], ALU.mult, ALU.mult
+            )
 
         fetch(0)
         fetch(1)
         take_larger(0)
-        fetch(2)
-        send(0)
         take_larger(1)
-        gate_and_weave(0)
+        send(0)
+        gate_beside(0)
+        fetch(2)
         send(1)
+        gate_beside(1)
         take_larger(2)
-        gate_and_weave(1)
         fetch(3)
         send(2)
-        take_larger(3)
-        gate_and_weave(2)
-        sig.append(keep.tile([P, H], F32, name="sig3", tag="z_plane2", align_bytes=64))
+        gate_beside(2)
+        sig.append(sbuf("sig3", [H], F32, "gated2"))
         nc.scalar.activation(sig[LAST][:], rows[LAST][:, 0:H], ACT.Sigmoid)
+        take_larger(3)
+        w1_q = quantize_w1(0, 1, "larger0")
         send(3)
-        w1_first = quantize("w1a", w1_grouped[:, 0 : P * PACK], P, tag="larger2")
-        z_last = keep.tile([P, HALF], BF16, name="z_last", tag="z_last", align_bytes=64)
-        gate(z_last[:], LAST, halves[0])
-        nc.scalar.copy(z_grouped[0][:, :, LAST], z_last[:])
-        gate(z_grouped[1][:, :, LAST], LAST, halves[1])
-        z_q = [quantize("z%d" % u, z_grouped[u][:].rearrange("p c j -> p (c j)"), HALF) for u in range(2)]
-        w1_second = quantize("w1b", w1_grouped[:, P * PACK : 2 * P * PACK], P, tag="z_last")
-        w1_rest = quantize("w1c", w1_grouped[:, 2 * P * PACK :], 2 * P, tag="z_plane2")
+        w1_q = w1_q + quantize_w1(1, 1, "fetched1")
 
-        h_first = [psum.tile([P, HALF], F32, name="h_first%d" % u) for u in range(2)]
-        product(h_first[0][:], w1_first, slice(0, P), z_q[0])
-        nc.scalar.copy(rows[0][:, halves[0]], h_first[0][:])
-        product(h_first[1][:], w1_first, slice(0, P), z_q[1])
-        nc.vector.tensor_copy(rows[0][:, halves[1]], h_first[1][:])
-        stationary = [None, (w1_second, slice(0, P)), (w1_rest, slice(0, P)), (w1_rest, slice(P, 2 * P))]
-        h_tags = [None, "h_bank1", "y_bank1", "y_bank2"]
+        z_last = sbuf("z_last", [H // 2], BF16)
+        gate_last(z_last[:], HALVES[0])
+        nc.scalar.copy(z_grouped[0][:, :, LAST], z_last[:])
+        for cols in QUARTERS[2:]:
+            gate_last(z_grouped[1][:, cols.start - H // 2 : cols.stop - H // 2, LAST], cols)
+        z_codes = sbuf("z_codes", [H], U32)
+        z_scale = sbuf("z_scale", [H], U8)
+        z_pieces = [QUARTERS[2], HALVES[0], QUARTERS[3]]
+        for cols in z_pieces:
+            u = cols.start // (H // 2)
+            grouped = z_grouped[u][:, cols.start - HALVES[u].start : cols.stop - HALVES[u].start, :]
+            quantize(z_codes[:, cols], z_scale[:, cols], grouped.rearrange("p c j -> p (c j)"))
+        w1_q = w1_q + quantize_w1(2, 2, "gated2")
+
+        for u, cols in enumerate(z_pieces):
+            h_piece = psum.tile([P, cols.stop - cols.start], F32, name="h_piece%d" % u, tag="chunk%d" % u)
+            product(h_piece[:], w1_q[0][0], w1_q[0][1], z_codes[:, cols], z_scale[:, cols])
+            nc.scalar.copy(rows[0][:, cols], h_piece[:])
         for t in range(1, PACK):
-            h_bank = psum.tile([P, H], F32, name="h_bank%d" % t, tag=h_tags[t])
-            for u in range(2):
-                product(h_bank[:, halves[u]], stationary[t][0], stationary[t][1], z_q[u])
+            h_bank = psum.tile([P, H], F32, name="h_bank%d" % t, tag="bank%d" % t)
+            product(h_bank[:], w1_q[t][0], w1_q[t][1], z_codes[:], z_scale[:])
             nc.scalar.copy(rows[t][:, 0:H], h_bank[:])
 
-        minus = [keep.tile([P, H], F32, name="minus%d" % t) for t in range(PACK)]
-        result = [keep.tile([P, H], F32, name="result%d" % t) for t in range(PACK)]
+        minus = [sbuf("minus%d" % t, [H], F32) for t in range(PACK)]
+        result = [sbuf("result%d" % t, [H], F32) for t in range(PACK)]
         out_rows = out.rearrange("(p t) c -> p t c", t=PACK)
 
         def fetch_minus(t):
             nc.vector.tensor_copy(minus[t][:], rows[t][:].indirect(n4_t[:]))
 
-        def gap(t, lo, hi):
-            nc.vector.tensor_tensor(
-                result[t][:, lo:hi],
-                rows[t][:].indirect(n3_t[:, lo // 16 : hi // 16]),
-                minus[t][:, lo:hi],
-                ALU.subtract,
-            )
-            nc.sync.dma_start(out_rows[:, t, lo:hi], result[t][:, lo:hi])
+        def gap(t, cols):
+            offsets = n3_t[:, cols.start // LIST_ROWS : cols.stop // LIST_ROWS]
+            nc.vector.tensor_tensor(result[t][:, cols], rows[t][:].indirect(offsets), minus[t][:, cols], ALU.subtract)
+            nc.sync.dma_start(out_rows[:, t, cols], result[t][:, cols])
 
         fetch_minus(0)
-        fetch_minus(1)
-        gap(0, 0, H)
-        fetch_minus(2)
-        gap(1, 0, H)
-        fetch_minus(3)
-        gap(2, 0, H)
-        gap(3, 0, HALF)
-        gap(3, HALF, H)
+        for t in range(LAST):
+            fetch_minus(t + 1)
+            gap(t, slice(0, H))
+        for cols in HALVES:
+            gap(LAST, cols)

@@ -25,7 +25,6 @@ WINDOW = 2 * H
 HALVES = [slice(0, H // 2), slice(H // 2, H)]
 QUARTERS = [slice(c, c + H // 4) for c in range(0, H, H // 4)]
 WA_CHUNKS = [slice(0, 256), slice(256, 384), slice(384, 512)]
-GPSIMD_COLS = 96
 
 
 def tile_picked_toksendggap_none_p_kernel(
@@ -106,26 +105,23 @@ def tile_picked_toksendggap_none_p_kernel(
             grouped = sbuf("wa_grouped%d" % u, [(cols.stop - cols.start) * PACK], BF16)
             dst = grouped[:].rearrange("p (c i j) -> p c j i", i=4, j=PACK)
             src = wa_raw[u][:].rearrange("p j (c i) -> p c j i", i=4)
-            shared = GPSIMD_COLS // 4 if u == 0 else 0
-            if shared:
-                nc.gpsimd.tensor_scalar(dst[:, :shared], src[:, :shared], 1.0, 0.0, ALU.mult, ALU.add)
-            nc.scalar.copy(dst[:, shared:], src[:, shared:])
+            nc.scalar.copy(dst, src)
             quantize(wa_codes[:, cols], wa_scale[:, cols], grouped[:])
 
-        rows = [sbuf("rows%d" % t, [WINDOW], F32) for t in range(PACK)]
+        y_rows = [sbuf("y_rows%d" % t, [WINDOW], F32) for t in range(PACK)]
         for u, cols in enumerate(WA_CHUNKS):
             y_chunk = psum.tile([P, cols.stop - cols.start], F32, name="y_chunk%d" % u, tag="chunk%d" % u)
             product(y_chunk[:], x_codes[:, 0:P], x_scale[:, 0:P], wa_codes[:, cols], wa_scale[:, cols])
-            nc.scalar.copy(rows[0][:, cols], y_chunk[:])
+            nc.scalar.copy(y_rows[0][:, cols], y_chunk[:])
         y_bank = {}
         for t in range(1, PACK):
             tokens = slice(t * P, (t + 1) * P)
             y_bank[t] = psum.tile([P, H], F32, name="y_bank%d" % t, tag="bank%d" % t)
             product(y_bank[t][:], x_codes[:, tokens], x_scale[:, tokens], wa_codes[:], wa_scale[:])
-            nc.scalar.copy(rows[t][:, 0:H], y_bank[t][:])
+            nc.scalar.copy(y_rows[t][:, 0:H], y_bank[t][:])
         sig = [sbuf("sig%d" % t, [H], F32) for t in range(LAST)]
         for t in range(LAST):
-            nc.scalar.activation(sig[t][:], rows[t][:, 0:H], ACT.Sigmoid)
+            nc.scalar.activation(sig[t][:], y_rows[t][:, 0:H], ACT.Sigmoid)
 
         w1_grouped = sbuf("w1_grouped", [N * PACK], BF16)
         w1_dst = w1_grouped[:].rearrange("p (t m j) -> p m j t", t=PACK, j=PACK)
@@ -139,26 +135,25 @@ def tile_picked_toksendggap_none_p_kernel(
             quantize(codes[:], scales[:], w1_grouped[:, first * P * PACK : (first + count) * P * PACK])
             return [(codes[:, c * P : (c + 1) * P], scales[:, c * P : (c + 1) * P]) for c in range(count)]
 
-        fetched, larger = {}, {}
-        sent = [sbuf("sent%d" % t, [WINDOW], F32) for t in range(PACK)]
+        fetched = [sbuf("fetched%d" % t, [H], F32) for t in range(PACK)]
+        larger = [sbuf("larger%d" % t, [H], F32) for t in range(PACK)]
+        sent = {}
         z_grouped = [sbuf("z_grouped%d" % u, [H // 2, PACK], BF16) for u in range(2)]
 
         def fetch(t):
-            fetched[t] = sbuf("fetched%d" % t, [H], F32, "fetched%d" % (t % 2))
-            nc.vector.tensor_copy(fetched[t][:], rows[t][:].indirect(n2_t[:]))
+            nc.vector.tensor_copy(fetched[t][:], y_rows[t][:].indirect(n2_t[:]))
 
         def take_larger(t):
-            larger[t] = sbuf("larger%d" % t, [H], F32, "larger%d" % (t % 2))
-            nc.vector.tensor_tensor(larger[t][:], fetched[t][:], y_bank[t][:] if t else rows[0][:, 0:H], ALU.max)
+            nc.vector.tensor_tensor(larger[t][:], fetched[t][:], y_bank[t][:] if t else y_rows[0][:, 0:H], ALU.max)
 
         def send(t):
+            sent[t] = sbuf("sent%d" % t, [WINDOW], F32, "" if t else "y_rows%d" % LAST)
             nc.vector.tensor_copy(sent[t][:].indirect(n1_t[:]), larger[t][:])
 
-        def gate_beside(t):
-            gated = sbuf("gated%d" % t, [H], F32)
-            for u, cols in enumerate(HALVES):
-                nc.gpsimd.tensor_tensor(gated[:, cols], sent[t][:, cols], sig[t][:, cols], ALU.mult)
-                nc.scalar.activation(z_grouped[u][:, :, t], gated[:, cols], ACT.Copy, scale=gt_t[:, t : t + 1])
+        def gate_beside(t, u):
+            gated = sbuf("gated%d_%d" % (t, u), [H // 2], F32)
+            nc.gpsimd.tensor_tensor(gated[:], sent[t][:, HALVES[u]], sig[t][:, HALVES[u]], ALU.mult)
+            nc.scalar.activation(z_grouped[u][:, :, t], gated[:], ACT.Copy, scale=gt_t[:, t : t + 1])
 
         def gate_last(dst, cols):
             nc.vector.scalar_tensor_tensor(
@@ -166,24 +161,21 @@ def tile_picked_toksendggap_none_p_kernel(
             )
 
         fetch(0)
-        fetch(1)
-        take_larger(0)
-        take_larger(1)
-        send(0)
-        gate_beside(0)
-        fetch(2)
-        send(1)
-        gate_beside(1)
-        take_larger(2)
-        fetch(3)
-        send(2)
-        gate_beside(2)
-        sig.append(sbuf("sig3", [H], F32, "gated2"))
-        nc.scalar.activation(sig[LAST][:], rows[LAST][:, 0:H], ACT.Sigmoid)
-        take_larger(3)
-        w1_q = quantize_w1(0, 1, "larger0")
-        send(3)
-        w1_q = w1_q + quantize_w1(1, 1, "fetched1")
+        for t in range(LAST):
+            fetch(t + 1)
+            take_larger(t)
+        take_larger(LAST)
+        for t in range(LAST - 1):
+            send(t)
+            gate_beside(t, 1)
+            gate_beside(t, 0)
+        send(LAST - 1)
+        gate_beside(LAST - 1, 1)
+        sig.append(sbuf("sig3", [H], F32, "gated2_1"))
+        nc.scalar.activation(sig[LAST][:], y_bank[LAST][:], ACT.Sigmoid)
+        gate_beside(LAST - 1, 0)
+        send(LAST)
+        w1_q = quantize_w1(0, 2, "larger3")
 
         z_last = sbuf("z_last", [H // 2], BF16)
         gate_last(z_last[:], HALVES[0])
@@ -197,27 +189,28 @@ def tile_picked_toksendggap_none_p_kernel(
             u = cols.start // (H // 2)
             grouped = z_grouped[u][:, cols.start - HALVES[u].start : cols.stop - HALVES[u].start, :]
             quantize(z_codes[:, cols], z_scale[:, cols], grouped.rearrange("p c j -> p (c j)"))
-        w1_q = w1_q + quantize_w1(2, 2, "gated2")
+        w1_q = w1_q + quantize_w1(2, 2, "gated2_1")
 
+        h_rows = [sbuf("h_rows%d" % t, [WINDOW], F32) for t in range(PACK)]
         for u, cols in enumerate(z_pieces):
             h_piece = psum.tile([P, cols.stop - cols.start], F32, name="h_piece%d" % u, tag="chunk%d" % u)
             product(h_piece[:], w1_q[0][0], w1_q[0][1], z_codes[:, cols], z_scale[:, cols])
-            nc.scalar.copy(rows[0][:, cols], h_piece[:])
+            nc.scalar.copy(h_rows[0][:, cols], h_piece[:])
         for t in range(1, PACK):
             h_bank = psum.tile([P, H], F32, name="h_bank%d" % t, tag="bank%d" % t)
             product(h_bank[:], w1_q[t][0], w1_q[t][1], z_codes[:], z_scale[:])
-            nc.scalar.copy(rows[t][:, 0:H], h_bank[:])
+            nc.scalar.copy(h_rows[t][:, 0:H], h_bank[:])
 
         minus = [sbuf("minus%d" % t, [H], F32) for t in range(PACK)]
         result = [sbuf("result%d" % t, [H], F32) for t in range(PACK)]
         out_rows = out.rearrange("(p t) c -> p t c", t=PACK)
 
         def fetch_minus(t):
-            nc.vector.tensor_copy(minus[t][:], rows[t][:].indirect(n4_t[:]))
+            nc.vector.tensor_copy(minus[t][:], h_rows[t][:].indirect(n4_t[:]))
 
         def gap(t, cols):
             offsets = n3_t[:, cols.start // LIST_ROWS : cols.stop // LIST_ROWS]
-            nc.vector.tensor_tensor(result[t][:, cols], rows[t][:].indirect(offsets), minus[t][:, cols], ALU.subtract)
+            nc.vector.tensor_tensor(result[t][:, cols], h_rows[t][:].indirect(offsets), minus[t][:, cols], ALU.subtract)
             nc.sync.dma_start(out_rows[:, t, cols], result[t][:, cols])
 
         fetch_minus(0)

from contextlib import ExitStack

import concourse.mybir as mybir

K, T, S, N, H = 512, 2048, 512, 512, 512
FLOPS = 2 * K * S * H + 2 * S * N * H

F32 = mybir.dt.float32
BF16 = mybir.dt.bfloat16
I32 = mybir.dt.int32
U32 = mybir.dt.uint32
U16 = mybir.dt.uint16
U8 = mybir.dt.uint8
FP8X4 = mybir.dt.float8_e4m3fn_x4
ALU = mybir.AluOpType
ACT = mybir.ActivationFunctionType

P = 128
PACK = 4
LAST = PACK - 1
QUADRANT = 32
LIST_ROWS = 16
ALIGN = 64
WINDOW = 2 * H
HALVES = [slice(0, H // 2), slice(H // 2, H)]
QUARTERS = [slice(c, c + H // 4) for c in range(0, H, H // 4)]
WA_CHUNKS = [slice(0, 256), slice(256, 384), slice(384, 512)]


def tile_picked_toksendggap_none_p_kernel(
    tc, x_words, x_scales, wa, gt, w1, offs, n1, n2, n3, n4, out
):
    nc = tc.nc
    with ExitStack() as ctx:
        lists = ctx.enter_context(tc.tile_pool(name="lists", bufs=1))
        keep = ctx.enter_context(tc.tile_pool(name="keep", bufs=1))
        psum = ctx.enter_context(tc.psum_pool(name="psum", bufs=1))

        def sbuf(name, shape, dtype, tag=""):
            return keep.tile([P] + shape, dtype, name=name, tag=tag or name, align_bytes=ALIGN)

        def load_list(name, src):
            tile = lists.tile([P, S // LIST_ROWS], U16, name=name)
            nc.sync.dma_start(tile[:], src)
            return tile

        def scale_partitions(q):
            return slice(QUADRANT * q, QUADRANT * q + 4)

        def quantize(codes, scales, grouped):
            nc.vector.quantize_mx(out=codes.bitcast(FP8X4), scales=scales, in_=grouped)

        def product(bank, lhs_codes, lhs_scales, rhs_codes, rhs_scales):
            nc.tensor.matmul_mx(
                out=bank,
                lhsT=lhs_codes.bitcast(FP8X4),
                lhsT_scale=lhs_scales,
                rhs=rhs_codes.bitcast(FP8X4),
                rhs_scale=rhs_scales,
                start=True,
                stop=True,
            )

        scale_table = sbuf("scale_table", [T], U8)
        nc.vector.memset(scale_table[:].bitcast(I32), 0)
        warm = sbuf("warm", [8], F32)
        nc.vector.memset(warm[:, 0:1], 0.0)

        scale_rows = sbuf("scale_rows", [T // 4], I32)
        for q in range(4):
            nc.sync.dma_start(scale_rows[scale_partitions(q), :], x_scales[0, 4 * q : 4 * q + 4, :].bitcast(I32))
        word_table = sbuf("word_table", [T], U32)
        nc.sync.dma_start(word_table[:].bitcast(I32), x_words[0].rearrange("p n t -> p (n t)").bitcast(I32))
        offs_t = load_list("offs_t", offs)
        wa_rows = wa.rearrange("(p j) c -> p j c", j=PACK)
        wa_raw = []
        for u, cols in enumerate(WA_CHUNKS):
            wa_raw.append(sbuf("wa_raw%d" % u, [PACK, cols.stop - cols.start], F32))
            nc.sync.dma_start(wa_raw[u][:], wa_rows[:, :, cols])
        n2_t = load_list("n2_t", n2)
        n1_t = load_list("n1_t", n1)
        gt_t = sbuf("gt_t", [PACK], F32)
        nc.sync.dma_start(gt_t[:], gt.rearrange("(p t) o -> p (t o)", t=PACK))
        w1_raw = sbuf("w1_raw", [PACK, N], F32)
        nc.sync.dma_start(w1_raw[:], w1.rearrange("(p j) c -> p j c", j=PACK))
        n4_t = load_list("n4_t", n4)
        n3_t = load_list("n3_t", n3)

        nc.scalar.activation(warm[:, 4:5], warm[:, 0:1], ACT.Sigmoid)

        for q in range(4):
            nc.vector.tensor_copy(scale_table[scale_partitions(q), :].bitcast(I32), scale_rows[scale_partitions(q), :])
        picked_scales = sbuf("picked_scales", [S], U8)
        nc.vector.tensor_copy(picked_scales[:], scale_table[:].indirect(offs_t[:]))
        x_codes = sbuf("x_codes", [S], U32)
        nc.vector.tensor_copy(x_codes[:].rearrange("p (t m) -> p m t", t=PACK), word_table[:].indirect(offs_t[:]))
        x_scale = sbuf("x_scale", [S], U8)
        nc.vector.tensor_copy(
            x_scale[:].rearrange("p (t m) -> p t m", t=PACK), picked_scales[:].rearrange("p (m t) -> p t m", t=PACK)
        )

        wa_codes = sbuf("wa_codes", [H], U32)
        wa_scale = sbuf("wa_scale", [H], U8)
        for u, cols in enumerate(WA_CHUNKS):
            grouped = sbuf("wa_grouped%d" % u, [(cols.stop - cols.start) * PACK], BF16)
            dst = grouped[:].rearrange("p (c i j) -> p c j i", i=4, j=PACK)
            src = wa_raw[u][:].rearrange("p j (c i) -> p c j i", i=4)
            nc.scalar.copy(dst, src)
            quantize(wa_codes[:, cols], wa_scale[:, cols], grouped[:])

        y_rows = [sbuf("y_rows%d" % t, [WINDOW], F32) for t in range(PACK)]
        for u, cols in enumerate(WA_CHUNKS):
            y_chunk = psum.tile([P, cols.stop - cols.start], F32, name="y_chunk%d" % u, tag="chunk%d" % u)
            product(y_chunk[:], x_codes[:, 0:P], x_scale[:, 0:P], wa_codes[:, cols], wa_scale[:, cols])
            nc.scalar.copy(y_rows[0][:, cols], y_chunk[:])
        y_bank = {}
        for t in range(1, PACK):
            tokens = slice(t * P, (t + 1) * P)
            y_bank[t] = psum.tile([P, H], F32, name="y_bank%d" % t, tag="bank%d" % t)
            product(y_bank[t][:], x_codes[:, tokens], x_scale[:, tokens], wa_codes[:], wa_scale[:])
            nc.scalar.copy(y_rows[t][:, 0:H], y_bank[t][:])
        sig = [sbuf("sig%d" % t, [H], F32) for t in range(LAST)]
        for t in range(LAST):
            nc.scalar.activation(sig[t][:], y_rows[t][:, 0:H], ACT.Sigmoid)

        w1_grouped = sbuf("w1_grouped", [N * PACK], BF16)
        w1_dst = w1_grouped[:].rearrange("p (t m j) -> p m j t", t=PACK, j=PACK)
        w1_src = w1_raw[:].rearrange("p j (m t) -> p m j t", t=PACK)
        for m0 in range(0, P, P // 2):
            nc.scalar.copy(w1_dst[:, m0 : m0 + P // 2], w1_src[:, m0 : m0 + P // 2])

        def quantize_w1(first, count, tag):
            codes = sbuf("w1_codes%d" % first, [count * P], U32, tag)
            scales = sbuf("w1_scale%d" % first, [count * P], U8)
            quantize(codes[:], scales[:], w1_grouped[:, first * P * PACK : (first + count) * P * PACK])
            return [(codes[:, c * P : (c + 1) * P], scales[:, c * P : (c + 1) * P]) for c in range(count)]

        fetched = [sbuf("fetched%d" % t, [H], F32) for t in range(PACK)]
        larger = [sbuf("larger%d" % t, [H], F32) for t in range(PACK)]
        sent = {}
        z_grouped = [sbuf("z_grouped%d" % u, [H // 2, PACK], BF16) for u in range(2)]

        def fetch(t):
            nc.vector.tensor_copy(fetched[t][:], y_rows[t][:].indirect(n2_t[:]))

        def take_larger(t):
            nc.vector.tensor_tensor(larger[t][:], fetched[t][:], y_bank[t][:] if t else y_rows[0][:, 0:H], ALU.max)

        def send(t):
            sent[t] = sbuf("sent%d" % t, [WINDOW], F32, "" if t else "y_rows%d" % LAST)
            nc.vector.tensor_copy(sent[t][:].indirect(n1_t[:]), larger[t][:])

        def gate_beside(t, u):
            gated = sbuf("gated%d_%d" % (t, u), [H // 2], F32)
            nc.gpsimd.tensor_tensor(gated[:], sent[t][:, HALVES[u]], sig[t][:, HALVES[u]], ALU.mult)
            nc.scalar.activation(z_grouped[u][:, :, t], gated[:], ACT.Copy, scale=gt_t[:, t : t + 1])

        def gate_last(dst, cols):
            nc.vector.scalar_tensor_tensor(
                dst, sent[LAST][:, cols], gt_t[:, LAST : LAST + 1], sig[LAST][:, cols], ALU.mult, ALU.mult
            )

        fetch(0)
        for t in range(LAST):
            fetch(t + 1)
            take_larger(t)
        take_larger(LAST)
        for t in range(LAST - 1):
            send(t)
            gate_beside(t, 1)
            gate_beside(t, 0)
        send(LAST - 1)
        gate_beside(LAST - 1, 1)
        sig.append(sbuf("sig3", [H], F32, "gated2_1"))
        nc.scalar.activation(sig[LAST][:], y_bank[LAST][:], ACT.Sigmoid)
        gate_beside(LAST - 1, 0)
        send(LAST)
        w1_q = quantize_w1(0, 2, "larger3")

        z_last = sbuf("z_last", [H // 2], BF16)
        gate_last(z_last[:], HALVES[0])
        nc.scalar.copy(z_grouped[0][:, :, LAST], z_last[:])
        for cols in QUARTERS[2:]:
            gate_last(z_grouped[1][:, cols.start - H // 2 : cols.stop - H // 2, LAST], cols)
        z_codes = sbuf("z_codes", [H], U32)
        z_scale = sbuf("z_scale", [H], U8)
        z_pieces = [QUARTERS[2], HALVES[0], QUARTERS[3]]
        for cols in z_pieces:
            u = cols.start // (H // 2)
            grouped = z_grouped[u][:, cols.start - HALVES[u].start : cols.stop - HALVES[u].start, :]
            quantize(z_codes[:, cols], z_scale[:, cols], grouped.rearrange("p c j -> p (c j)"))
        w1_q = w1_q + quantize_w1(2, 2, "gated2_1")

        h_rows = [sbuf("h_rows%d" % t, [WINDOW], F32) for t in range(PACK)]
        for u, cols in enumerate(z_pieces):
            h_piece = psum.tile([P, cols.stop - cols.start], F32, name="h_piece%d" % u, tag="chunk%d" % u)
            product(h_piece[:], w1_q[0][0], w1_q[0][1], z_codes[:, cols], z_scale[:, cols])
            nc.scalar.copy(h_rows[0][:, cols], h_piece[:])
        for t in range(1, PACK):
            h_bank = psum.tile([P, H], F32, name="h_bank%d" % t, tag="bank%d" % t)
            product(h_bank[:], w1_q[t][0], w1_q[t][1], z_codes[:], z_scale[:])
            nc.scalar.copy(h_rows[t][:, 0:H], h_bank[:])

        minus = [sbuf("minus%d" % t, [H], F32) for t in range(PACK)]
        result = [sbuf("result%d" % t, [H], F32) for t in range(PACK)]
        out_rows = out.rearrange("(p t) c -> p t c", t=PACK)

        def fetch_minus(t):
            nc.vector.tensor_copy(minus[t][:], h_rows[t][:].indirect(n4_t[:]))

        def gap(t, cols):
            offsets = n3_t[:, cols.start // LIST_ROWS : cols.stop // LIST_ROWS]
            nc.vector.tensor_tensor(result[t][:, cols], h_rows[t][:].indirect(offsets), minus[t][:, cols], ALU.subtract)
            nc.sync.dma_start(out_rows[:, t, cols], result[t][:, cols])

        fetch_minus(0)
        for t in range(LAST):
            fetch_minus(t + 1)
            gap(t, slice(0, H))
        for cols in HALVES:
            gap(LAST, cols)
